import numpy as np
import ml_dtypes


def mxq(x, axis, fmt="e4m3"):
    dtype, down = {"e4m3": (ml_dtypes.float8_e4m3fn, 7), "e5m2": (ml_dtypes.float8_e5m2, 14)}[fmt]
    v = np.moveaxis(np.asarray(x, np.float32).astype(ml_dtypes.bfloat16).astype(np.float64), axis, -1)
    blocks = v.reshape(v.shape[:-1] + (-1, 32))
    amax = np.abs(blocks).max(-1, keepdims=True)
    byte = np.maximum(np.where(amax > 0, np.frexp(amax)[1] - 1 + 127, 0) - down, 1)
    scale = np.exp2(byte - 127.0)
    codes = (blocks / scale).astype(np.float32).astype(dtype).astype(np.float64)
    return np.moveaxis((codes * scale).reshape(v.shape), -1, axis)


WIDE = False


def mx_kscale(k):
    if not WIDE:
        return np.ones(k)
    levels = np.array([30, -30])
    if k % 512:
        return np.exp2(np.random.permutation(np.resize(levels, k // 32))).repeat(32)
    a = np.empty((k // 512, 16))
    for p in range(k // 512):
        a[p, :8] = np.random.permutation(np.resize(levels, 8))
        for g in range(8):
            far = levels[np.abs(levels - a[p, g]) >= 10]
            a[p, g + 8] = far[np.random.randint(len(far))]
    return np.exp2(a.ravel()).repeat(32)


def f64(x):
    return np.asarray(x).astype(np.float64)


E2M1 = np.array([0.0, 0.5, 1.0, 1.5, 2.0, 3.0, 4.0, 6.0, -0.0, -0.5, -1.0, -1.5, -2.0, -3.0, -4.0, -6.0])


def pack_weight(w, fmt):
    k, n = w.shape
    w = f64(np.asarray(w, np.float32).astype(ml_dtypes.bfloat16)).reshape(k // 32, 32, n)
    amax = np.abs(w).max(1)
    if fmt == "e4m3":
        byte = np.frexp(amax)[1] - 1 + 127 - 7
    else:
        mant, ex = np.frexp(amax / 6.0)
        byte = np.where(mant > 0.5, ex, ex - 1) + 127
    byte = np.clip(np.where(amax > 0, byte, 1), 1, 254)
    scaled = (w * np.exp2(127.0 - byte)[:, None, :]).reshape(k, n).astype(np.float32)
    by_word = np.ascontiguousarray(scaled.reshape(k // 512, 128, 4, n).transpose(0, 1, 3, 2))
    if fmt == "e4m3":
        words = by_word.astype(ml_dtypes.float8_e4m3fn).view(np.uint8)
    else:
        c = by_word.astype(ml_dtypes.float4_e2m1fn).view(np.uint8) & 0xF
        words = (c[..., 0::2] | (c[..., 1::2] << 4)).reshape(k // 512, 128, 2 * n)
    return np.ascontiguousarray(words), np.ascontiguousarray(byte.astype(np.uint8).reshape(k // 512, 16, n))


def unpack_weight(words, scales, fmt):
    g, _, n = scales.shape
    words = np.ascontiguousarray(words).reshape(g, 128, n, -1)
    if fmt == "e4m3":
        vals = words.view(ml_dtypes.float8_e4m3fn).astype(np.float64)
    else:
        nib = np.empty((g, 128, n, 4), np.uint8)
        nib[..., 0::2] = words & 0xF
        nib[..., 1::2] = words >> 4
        vals = E2M1[nib]
    vals = vals * np.repeat(np.exp2(scales.astype(np.float64) - 127.0), 8, axis=1)[..., None]
    return vals.transpose(0, 1, 3, 2).reshape(g * 512, n)


O, K, M, T = 1024, 1536, 512, 1536


def setup_inputs():
    n = np.random.standard_normal
    s = mx_kscale(K)[:, None]
    dy = np.exp(0.5 * n((1, T))) * n((K, T))
    w = n((K, M)) / np.sqrt(K) / s
    p_w8 = pack_weight(w[:O], "e4m3")
    p_w4 = pack_weight(w[O:], "e2m1")
    return {
        "dy": (dy * s).astype(np.float32),
        "w8_words": p_w8[0],
        "w8_scales": p_w8[1],
        "w4_words": p_w4[0],
        "w4_scales": p_w4[1],
        "g": (n((1536, 512))).astype(np.float32),
    }


def reference(dy, w8_words, w8_scales, w4_words, w4_scales, g):
    dy_ = mxq(f64(dy), 0, "e5m2")
    w8_ = unpack_weight(w8_words, w8_scales, "e4m3")
    w4_ = unpack_weight(w4_words, w4_scales, "e2m1")
    y = dy_[:O].T @ w8_ + dy_[O:].T @ w4_
    return f64(g) * y

@@ -1,0 +1,119 @@
+from contextlib import ExitStack
+
+import concourse.mybir as mybir
+
+F32 = mybir.dt.float32
+BF16 = mybir.dt.bfloat16
+U32 = mybir.dt.uint32
+I32 = mybir.dt.int32
+U8 = mybir.dt.uint8
+E4M3X4 = mybir.dt.float8_e4m3fn_x4
+E5M2X4 = mybir.dt.float8_e5m2_x4
+E2M1X4 = mybir.dt.float4_e2m1fn_x4
+MULT = mybir.AluOpType.mult
+
+P = 128
+K, T, D = 1536, 1536, 512
+PASSES = 3
+TILES = T // P
+QUADS = TILES // 4
+
+FLOPS = 2 * K * T * D
+BYTES = 4 * K * T + 2 * 4 * T * D + 1024 * D + 512 * D // 2 + 48 * D
+
+STORES = ((0, 4), (4, 6), (6, 8), (8, 10), (10, 11), (11, 12))
+SPLIT = 64
+
+
+def tile_mix_dyq_tm_mul_kernel(tc, dy, w8_words, w8_scales, w4_words, w4_scales, g, out):
+    nc = tc.nc
+    with ExitStack() as ctx:
+        keep = ctx.enter_context(tc.tile_pool(name="keep", bufs=1))
+        psum = ctx.enter_context(tc.psum_pool(name="psum", bufs=1))
+        ctx.enter_context(tc.manual_schedule())
+
+        planes = keep.tile([P, PASSES, D], U8, name="planes", align_bytes=64)
+        w8 = keep.tile([P, 2, D], U32, name="w8", align_bytes=64)
+        w4 = keep.tile([P, 2 * D], U8, name="w4", align_bytes=64)
+        raw = [keep.tile([P, 4, T], F32, name="raw%d" % a, align_bytes=64) for a in range(PASSES)]
+        g_sb = keep.tile([P, TILES, D], F32, name="g_sb", align_bytes=64)
+        o_sb = keep.tile([P, TILES, D], F32, name="o_sb", align_bytes=64)
+        grouped = {}
+        codes = {}
+        scales = {}
+        for a in range(PASSES):
+            for q in range(QUADS):
+                grouped[a, q] = keep.tile([P, 4 * D], BF16, name="grouped%d_%d" % (a, q), align_bytes=64)
+                codes[a, q] = keep.tile([P, D], U32, name="codes%d_%d" % (a, q), align_bytes=64)
+                scales[a, q] = keep.tile([P, D], U8, name="scales%d_%d" % (a, q), align_bytes=64)
+
+        def load_dy(a):
+            nc.sync.dma_start(out=raw[a][:], in_=dy[512 * a : 512 * (a + 1), :].rearrange("(p j) t -> p j t", j=4))
+
+        nc.vector.memset(planes[:].bitcast(I32), 0)
+        load_dy(0)
+        for b in range(4):
+            nc.sync.dma_start(
+                out=planes[32 * b : 32 * b + 4, 0:2, :].bitcast(I32),
+                in_=w8_scales[:, 4 * b : 4 * b + 4, :].rearrange("a r n -> r a n").bitcast(I32),
+            )
+        nc.sync.dma_start(out=w8[:].bitcast(I32), in_=w8_words.rearrange("a p n t -> p a (n t)").bitcast(I32))
+        nc.sync.dma_start(out=w4[:].bitcast(I32), in_=w4_words[0].bitcast(I32))
+        load_dy(1)
+        for b in range(4):
+            nc.sync.dma_start(
+                out=planes[32 * b : 32 * b + 4, 2, :].bitcast(I32),
+                in_=w4_scales[0, 4 * b : 4 * b + 4, :].bitcast(I32),
+            )
+        load_dy(2)
+        g_view = g.rearrange("(p r) d -> p r d", r=TILES)
+        out_view = out.rearrange("(p r) d -> p r d", r=TILES)
+        for q in range(QUADS):
+            rows = slice(4 * q, 4 * q + 4)
+            nc.sync.dma_start(out=g_sb[:, rows, :], in_=g_view[:, rows, :])
+
+
+        def group(copy, a, q, m0, m1):
+            src = raw[a][:].rearrange("p j (m q i) -> p q m j i", q=QUADS, i=4)[:, q]
+            dst = grouped[a, q][:].rearrange("p (i m j) -> p m j i", i=4, j=4)
+            copy(out=dst[:, m0:m1], in_=src[:, m0:m1])
+
+        def quantise(a, q):
+            nc.vector.quantize_mx(out=codes[a, q][:].bitcast(E5M2X4), scales=scales[a, q][:], in_=grouped[a, q][:])
+
+        acc = {}
+
+        def multiply(a, r):
+            if a == 0:
+                acc[r] = psum.tile([P, D], F32, name="acc%d" % (r % 8))
+            cols = slice(P * (r % 4), P * (r % 4 + 1))
+            nc.tensor.matmul_mx(
+                out=acc[r][:],
+                lhsT=codes[a, r // 4][:, cols].bitcast(E5M2X4),
+                lhsT_scale=scales[a, r // 4][:, cols],
+                rhs=w8[:, a, :].bitcast(E4M3X4) if a < 2 else w4[:].bitcast(E2M1X4),
+                rhs_scale=planes[:, a, :],
+                start=(a == 0),
+                stop=(a == PASSES - 1),
+            )
+
+        for a in range(PASSES):
+            group(nc.scalar.copy, a, 1, SPLIT, P)
+            group(nc.scalar.copy, a, 2, 0, P)
+            group(nc.vector.tensor_copy, a, 0, 0, P)
+            group(nc.vector.tensor_copy, a, 1, 0, SPLIT)
+            for q in range(QUADS):
+                quantise(a, q)
+            for r in range(8):
+                multiply(a, r)
+
+        def finish(r):
+            nc.vector.tensor_tensor(out=o_sb[:, r, :], in0=acc[r][:], in1=g_sb[:, r, :], op=MULT)
+
+        for lo, hi in STORES:
+            for r in range(lo, hi):
+                finish(r)
+                if r + 8 < TILES:
+                    for a in range(PASSES):
+                        multiply(a, r + 8)
+            nc.sync.dma_start(out=out_view[:, lo:hi, :], in_=o_sb[:, lo:hi, :])

@@ -21,8 +21,7 @@ QUADS = TILES // 4
 FLOPS = 2 * K * T * D
 BYTES = 4 * K * T + 2 * 4 * T * D + 1024 * D + 512 * D // 2 + 48 * D
 
-STORES = ((0, 4), (4, 6), (6, 8), (8, 10), (10, 11), (11, 12))
-SPLIT = 64
+STORES = ((4, 6), (6, 8), (8, 10), (10, 11), (11, 12))
 
 
 def tile_mix_dyq_tm_mul_kernel(tc, dy, w8_words, w8_scales, w4_words, w4_scales, g, out):
@@ -58,14 +57,14 @@ def tile_mix_dyq_tm_mul_kernel(tc, dy, w8_words, w8_scales, w4_words, w4_scales,
                 in_=w8_scales[:, 4 * b : 4 * b + 4, :].rearrange("a r n -> r a n").bitcast(I32),
             )
         nc.sync.dma_start(out=w8[:].bitcast(I32), in_=w8_words.rearrange("a p n t -> p a (n t)").bitcast(I32))
-        nc.sync.dma_start(out=w4[:].bitcast(I32), in_=w4_words[0].bitcast(I32))
         load_dy(1)
+        load_dy(2)
         for b in range(4):
             nc.sync.dma_start(
                 out=planes[32 * b : 32 * b + 4, 2, :].bitcast(I32),
                 in_=w4_scales[0, 4 * b : 4 * b + 4, :].bitcast(I32),
             )
-        load_dy(2)
+        nc.sync.dma_start(out=w4[:].bitcast(I32), in_=w4_words[0].bitcast(I32))
         g_view = g.rearrange("(p r) d -> p r d", r=TILES)
         out_view = out.rearrange("(p r) d -> p r d", r=TILES)
         for q in range(QUADS):
@@ -97,23 +96,39 @@ def tile_mix_dyq_tm_mul_kernel(tc, dy, w8_words, w8_scales, w4_words, w4_scales,
                 stop=(a == PASSES - 1),
             )
 
-        for a in range(PASSES):
-            group(nc.scalar.copy, a, 1, SPLIT, P)
-            group(nc.scalar.copy, a, 2, 0, P)
-            group(nc.vector.tensor_copy, a, 0, 0, P)
-            group(nc.vector.tensor_copy, a, 1, 0, SPLIT)
-            for q in range(QUADS):
-                quantise(a, q)
-            for r in range(8):
-                multiply(a, r)
-
         def finish(r):
             nc.vector.tensor_tensor(out=o_sb[:, r, :], in0=acc[r][:], in1=g_sb[:, r, :], op=MULT)
 
+        def store(lo, hi):
+            nc.sync.dma_start(out=out_view[:, lo:hi, :], in_=o_sb[:, lo:hi, :])
+
+        for a in range(PASSES):
+            group(nc.scalar.copy, a, 1, 0, P)
+            group(nc.scalar.copy, a, 2, 0, P)
+            group(nc.vector.tensor_copy, a, 0, 0, P)
+            quantise(a, 0)
+            if a < PASSES - 1:
+                quantise(a, 1)
+                quantise(a, 2)
+                for r in range(8):
+                    multiply(a, r)
+
+        for r in range(4):
+            multiply(2, r)
+        for r in range(4):
+            finish(r)
+            if r == 0:
+                quantise(2, 1)
+                for s in range(4, 8):
+                    multiply(2, s)
+            multiply(0, r + 8)
+            multiply(1, r + 8)
+            if r % 2:
+                store(r - 1, r + 1)
+        quantise(2, 2)
+        for r in range(8, TILES):
+            multiply(2, r)
         for lo, hi in STORES:
             for r in range(lo, hi):
                 finish(r)
-                if r + 8 < TILES:
-                    for a in range(PASSES):
-                        multiply(a, r + 8)
-            nc.sync.dma_start(out=out_view[:, lo:hi, :], in_=o_sb[:, lo:hi, :])
+            store(lo, hi)

from contextlib import ExitStack

import concourse.mybir as mybir

F32 = mybir.dt.float32
BF16 = mybir.dt.bfloat16
U32 = mybir.dt.uint32
I32 = mybir.dt.int32
U8 = mybir.dt.uint8
E4M3X4 = mybir.dt.float8_e4m3fn_x4
E5M2X4 = mybir.dt.float8_e5m2_x4
E2M1X4 = mybir.dt.float4_e2m1fn_x4
MULT = mybir.AluOpType.mult

P = 128
K, T, D = 1536, 1536, 512
PASSES = 3
TILES = T // P
QUADS = TILES // 4

FLOPS = 2 * K * T * D
BYTES = 4 * K * T + 2 * 4 * T * D + 1024 * D + 512 * D // 2 + 48 * D

STORES = ((4, 6), (6, 8), (8, 10), (10, 11), (11, 12))


def tile_mix_dyq_tm_mul_kernel(tc, dy, w8_words, w8_scales, w4_words, w4_scales, g, out):
    nc = tc.nc
    with ExitStack() as ctx:
        keep = ctx.enter_context(tc.tile_pool(name="keep", bufs=1))
        psum = ctx.enter_context(tc.psum_pool(name="psum", bufs=1))
        ctx.enter_context(tc.manual_schedule())

        planes = keep.tile([P, PASSES, D], U8, name="planes", align_bytes=64)
        w8 = keep.tile([P, 2, D], U32, name="w8", align_bytes=64)
        w4 = keep.tile([P, 2 * D], U8, name="w4", align_bytes=64)
        raw = [keep.tile([P, 4, T], F32, name="raw%d" % a, align_bytes=64) for a in range(PASSES)]
        g_sb = keep.tile([P, TILES, D], F32, name="g_sb", align_bytes=64)
        o_sb = keep.tile([P, TILES, D], F32, name="o_sb", align_bytes=64)
        grouped = {}
        codes = {}
        scales = {}
        for a in range(PASSES):
            for q in range(QUADS):
                grouped[a, q] = keep.tile([P, 4 * D], BF16, name="grouped%d_%d" % (a, q), align_bytes=64)
                codes[a, q] = keep.tile([P, D], U32, name="codes%d_%d" % (a, q), align_bytes=64)
                scales[a, q] = keep.tile([P, D], U8, name="scales%d_%d" % (a, q), align_bytes=64)

        def load_dy(a):
            nc.sync.dma_start(out=raw[a][:], in_=dy[512 * a : 512 * (a + 1), :].rearrange("(p j) t -> p j t", j=4))

        nc.vector.memset(planes[:].bitcast(I32), 0)
        load_dy(0)
        for b in range(4):
            nc.sync.dma_start(
                out=planes[32 * b : 32 * b + 4, 0:2, :].bitcast(I32),
                in_=w8_scales[:, 4 * b : 4 * b + 4, :].rearrange("a r n -> r a n").bitcast(I32),
            )
        nc.sync.dma_start(out=w8[:].bitcast(I32), in_=w8_words.rearrange("a p n t -> p a (n t)").bitcast(I32))
        load_dy(1)
        load_dy(2)
        for b in range(4):
            nc.sync.dma_start(
                out=planes[32 * b : 32 * b + 4, 2, :].bitcast(I32),
                in_=w4_scales[0, 4 * b : 4 * b + 4, :].bitcast(I32),
            )
        nc.sync.dma_start(out=w4[:].bitcast(I32), in_=w4_words[0].bitcast(I32))
        g_view = g.rearrange("(p r) d -> p r d", r=TILES)
        out_view = out.rearrange("(p r) d -> p r d", r=TILES)
        for q in range(QUADS):
            rows = slice(4 * q, 4 * q + 4)
            nc.sync.dma_start(out=g_sb[:, rows, :], in_=g_view[:, rows, :])


        def group(copy, a, q, m0, m1):
            src = raw[a][:].rearrange("p j (m q i) -> p q m j i", q=QUADS, i=4)[:, q]
            dst = grouped[a, q][:].rearrange("p (i m j) -> p m j i", i=4, j=4)
            copy(out=dst[:, m0:m1], in_=src[:, m0:m1])

        def quantise(a, q):
            nc.vector.quantize_mx(out=codes[a, q][:].bitcast(E5M2X4), scales=scales[a, q][:], in_=grouped[a, q][:])

        acc = {}

        def multiply(a, r):
            if a == 0:
                acc[r] = psum.tile([P, D], F32, name="acc%d" % (r % 8))
            cols = slice(P * (r % 4), P * (r % 4 + 1))
            nc.tensor.matmul_mx(
                out=acc[r][:],
                lhsT=codes[a, r // 4][:, cols].bitcast(E5M2X4),
                lhsT_scale=scales[a, r // 4][:, cols],
                rhs=w8[:, a, :].bitcast(E4M3X4) if a < 2 else w4[:].bitcast(E2M1X4),
                rhs_scale=planes[:, a, :],
                start=(a == 0),
                stop=(a == PASSES - 1),
            )

        def finish(r):
            nc.vector.tensor_tensor(out=o_sb[:, r, :], in0=acc[r][:], in1=g_sb[:, r, :], op=MULT)

        def store(lo, hi):
            nc.sync.dma_start(out=out_view[:, lo:hi, :], in_=o_sb[:, lo:hi, :])

        for a in range(PASSES):
            group(nc.scalar.copy, a, 1, 0, P)
            group(nc.scalar.copy, a, 2, 0, P)
            group(nc.vector.tensor_copy, a, 0, 0, P)
            quantise(a, 0)
            if a < PASSES - 1:
                quantise(a, 1)
                quantise(a, 2)
                for r in range(8):
                    multiply(a, r)

        for r in range(4):
            multiply(2, r)
        for r in range(4):
            finish(r)
            if r == 0:
                quantise(2, 1)
                for s in range(4, 8):
                    multiply(2, s)
            multiply(0, r + 8)
            multiply(1, r + 8)
            if r % 2:
                store(r - 1, r + 1)
        quantise(2, 2)
        for r in range(8, TILES):
            multiply(2, r)
        for lo, hi in STORES:
            for r in range(lo, hi):
                finish(r)
            store(lo, hi)
